import numpy as np
import ml_dtypes


def mxq(x, axis, fmt="e4m3"):
    dtype, down = {"e4m3": (ml_dtypes.float8_e4m3fn, 7), "e5m2": (ml_dtypes.float8_e5m2, 14)}[fmt]
    v = np.moveaxis(np.asarray(x, np.float32).astype(ml_dtypes.bfloat16).astype(np.float64), axis, -1)
    blocks = v.reshape(v.shape[:-1] + (-1, 32))
    amax = np.abs(blocks).max(-1, keepdims=True)
    byte = np.maximum(np.where(amax > 0, np.frexp(amax)[1] - 1 + 127, 0) - down, 1)
    scale = np.exp2(byte - 127.0)
    codes = (blocks / scale).astype(np.float32).astype(dtype).astype(np.float64)
    return np.moveaxis((codes * scale).reshape(v.shape), -1, axis)


WIDE = False


def mx_kscale(k):
    if not WIDE:
        return np.ones(k)
    levels = np.array([10, -10, 5, -5, 0])
    if k % 512:
        return np.exp2(np.random.permutation(np.resize(levels, k // 32))).repeat(32)
    a = np.empty((k // 512, 16))
    for p in range(k // 512):
        a[p, :8] = np.random.permutation(np.resize(levels, 8))
        for g in range(8):
            far = levels[np.abs(levels - a[p, g]) >= 10]
            a[p, g + 8] = far[np.random.randint(len(far))]
    return np.exp2(a.ravel()).repeat(32)


def f64(x):
    return np.asarray(x).astype(np.float64)


def striped(idx):
    return np.tile(np.asarray(idx).reshape(-1, 16).T, (8, 1)).astype(np.uint16)


def unstriped(offs):
    return offs[:16].T.reshape(-1).astype(np.int64)


E2M1 = np.array([0.0, 0.5, 1.0, 1.5, 2.0, 3.0, 4.0, 6.0, -0.0, -0.5, -1.0, -1.5, -2.0, -3.0, -4.0, -6.0])


def pack_weight(w, fmt):
    k, n = w.shape
    w = f64(np.asarray(w, np.float32).astype(ml_dtypes.bfloat16)).reshape(k // 32, 32, n)
    amax = np.abs(w).max(1)
    if fmt == "e4m3":
        byte = np.frexp(amax)[1] - 1 + 127 - 7
    else:
        mant, ex = np.frexp(amax / 6.0)
        byte = np.where(mant > 0.5, ex, ex - 1) + 127
    byte = np.clip(np.where(amax > 0, byte, 1), 1, 254)
    scaled = (w * np.exp2(127.0 - byte)[:, None, :]).reshape(k, n).astype(np.float32)
    by_word = np.ascontiguousarray(scaled.reshape(k // 512, 128, 4, n).transpose(0, 1, 3, 2))
    if fmt == "e4m3":
        words = by_word.astype(ml_dtypes.float8_e4m3fn).view(np.uint8)
    else:
        c = by_word.astype(ml_dtypes.float4_e2m1fn).view(np.uint8) & 0xF
        words = (c[..., 0::2] | (c[..., 1::2] << 4)).reshape(k // 512, 128, 2 * n)
    return np.ascontiguousarray(words), np.ascontiguousarray(byte.astype(np.uint8).reshape(k // 512, 16, n))


def unpack_weight(words, scales, fmt):
    g, _, n = scales.shape
    words = np.ascontiguousarray(words).reshape(g, 128, n, -1)
    if fmt == "e4m3":
        vals = words.view(ml_dtypes.float8_e4m3fn).astype(np.float64)
    else:
        nib = np.empty((g, 128, n, 4), np.uint8)
        nib[..., 0::2] = words & 0xF
        nib[..., 1::2] = words >> 4
        vals = E2M1[nib]
    vals = vals * np.repeat(np.exp2(scales.astype(np.float64) - 127.0), 8, axis=1)[..., None]
    return vals.transpose(0, 1, 3, 2).reshape(g * 512, n)


K, T, J, N = 512, 512, 512, 512


def setup_inputs():
    n = np.random.standard_normal
    idx = np.random.randint(0, T, J)
    idx2 = np.random.randint(0, T, J)
    fk = mx_kscale(K)
    xtp = pack_weight(n((K, T)) / fk[:, None], "e4m3")
    wbp = pack_weight(n((K, N)) * 1 / np.sqrt(K) * fk[:, None], "e2m1")
    return {
        "xt_words": xtp[0],
        "xt_scales": xtp[1],
        "wa": (n((K, N)) * 1 / np.sqrt(K) * fk[:, None]).astype(np.float32),
        "wb_words": wbp[0],
        "wb_scales": wbp[1],
        "offs": striped(idx),
        "offs2": striped(idx2),
    }


def reference(xt_words, xt_scales, wa, wb_words, wb_scales, offs, offs2):
    idx = unstriped(offs)
    idx2 = unstriped(offs2)
    xtu = unpack_weight(xt_words, xt_scales, "e4m3")
    wbu = unpack_weight(wb_words, wb_scales, "e2m1")
    waq = mxq(f64(wa), 0, "e4m3")
    za = waq.T @ xtu
    zb = wbu.T @ xtu
    d = za[:, idx] - zb[:, idx2]
    y = np.square(d) / (1.0 + np.abs(d))
    return y

@@ -1,0 +1,155 @@
+from contextlib import ExitStack
+
+import concourse.mybir as mybir
+
+K, T, J, N = 512, 512, 512, 512
+FLOPS = 2 * 2 * K * N * T
+
+F32 = mybir.dt.float32
+BF16 = mybir.dt.bfloat16
+I32 = mybir.dt.int32
+U32 = mybir.dt.uint32
+U16 = mybir.dt.uint16
+U8 = mybir.dt.uint8
+FP8X4 = mybir.dt.float8_e4m3fn_x4
+FP4X4 = mybir.dt.float4_e2m1fn_x4
+ACT = mybir.ActivationFunctionType
+ALU = mybir.AluOpType
+
+P = 128
+PACK = 4
+TILES = N // P
+ZA_COLS = 704
+ZB_COLS = 1024
+
+
+def load_scale_rows(queue, plane, rows):
+    for q in range(4):
+        queue.dma_start(out=plane[32 * q : 32 * q + 4, :].bitcast(I32), in_=rows[4 * q : 4 * q + 4, :].bitcast(I32))
+
+
+def tile_list_edge_difference_energy_kernel(tc, xt_words, xt_scales, wa, wb_words, wb_scales, offs, offs2, out):
+    nc = tc.nc
+    with ExitStack() as ctx:
+        keep = ctx.enter_context(tc.tile_pool(name="keep", bufs=1))
+        psum = ctx.enter_context(tc.psum_pool(name="psum", bufs=1))
+
+        tail_list = keep.tile([P, J // 16], U16, name="tail_list")
+        head_list = keep.tile([P, J // 16], U16, name="head_list")
+        x_codes = keep.tile([P, T], U32, name="x_codes", align_bytes=64)
+        x_plane = keep.tile([P, T], U8, name="x_plane", align_bytes=64)
+        b_codes = keep.tile([P, 2 * N], U8, name="b_codes", align_bytes=64)
+        b_plane = keep.tile([P, N], U8, name="b_plane", align_bytes=64)
+        warm = keep.tile([P, 2], F32, name="warm")
+
+        nc.vector.memset(x_plane[:].bitcast(I32), 0)
+        nc.vector.memset(b_plane[:].bitcast(I32), 0)
+        nc.vector.memset(warm[:, 0:1], 1.0)
+        load_scale_rows(nc.scalar, x_plane, xt_scales[0])
+        nc.scalar.activation(out=warm[:, 1:2], in_=warm[:, 0:1], func=ACT.Abs_reciprocal_sqrt)
+
+        wa_rows = wa.rearrange("(p j) n -> p j n", j=PACK)
+        raw0 = keep.tile([P, PACK, P], F32, name="raw0")
+        raw1 = keep.tile([P, PACK, P], F32, name="raw1")
+        raw23 = keep.tile([P, PACK, 2 * P], F32, name="raw23")
+        raws = [raw0[:], raw1[:], raw23[:, :, 0:P], raw23[:, :, P : 2 * P]]
+        nc.sync.dma_start(out=raw0[:], in_=wa_rows[:, :, 0:P])
+        nc.sync.dma_start(out=tail_list[:], in_=offs)
+        nc.sync.dma_start(out=x_codes[:].bitcast(I32), in_=xt_words[0].rearrange("p n t -> p (n t)").bitcast(I32))
+        nc.sync.dma_start(out=raw1[:], in_=wa_rows[:, :, P : 2 * P])
+        nc.sync.dma_start(out=raw23[:], in_=wa_rows[:, :, 2 * P : 4 * P])
+        load_scale_rows(nc.sync, b_plane, wb_scales[0])
+        nc.sync.dma_start(out=b_codes[:].bitcast(I32), in_=wb_words[0].bitcast(I32))
+        nc.sync.dma_start(out=head_list[:], in_=offs2)
+
+        za = [keep.tile([P, ZA_COLS], F32, name=f"za{w}") for w in range(2)]
+        zb = [keep.tile([P, ZB_COLS], F32, name=f"zb{w}") for w in range(2)]
+        for w in range(2):
+            nc.vector.memset(za[w][:, T:], 0.0)
+            nc.vector.memset(zb[w][:, T:], 0.0)
+
+        a_bank = ["p0", "p1", "p2", "p3"]
+        b_bank = ["p2", "p3", "p4", "p5"]
+        tails_slot = ["a", "b", "c", "c"]
+        diff_slot = ["c", "d", "d", "d"]
+        tails = {}
+
+        def tails_product(t):
+            grouped = keep.tile([P, P, PACK], BF16, name=f"grouped{t}", align_bytes=64)
+            (nc.vector.tensor_copy if t in [0] else nc.scalar.copy)(
+                out=grouped[:].rearrange("p (c i) j -> p c j i", i=4),
+                in_=raws[t].rearrange("p j (c i) -> p c j i", i=4),
+            )
+            a_codes = keep.tile([P, P], U32, name=f"a_codes{t}", align_bytes=64)
+            a_plane = keep.tile([P, P], U8, name=f"a_plane{t}", align_bytes=64)
+            nc.vector.quantize_mx(
+                out=a_codes[:].bitcast(FP8X4), scales=a_plane[:], in_=grouped[:].rearrange("p n j -> p (n j)")
+            )
+            acc_a = psum.tile([P, T], F32, name="acc_a", tag=a_bank[t])
+            nc.tensor.matmul_mx(
+                out=acc_a[:],
+                lhsT=a_codes[:].bitcast(FP8X4),
+                lhsT_scale=a_plane[:],
+                rhs=x_codes[:].bitcast(FP8X4),
+                rhs_scale=x_plane[:],
+                start=True,
+                stop=True,
+            )
+            nc.scalar.activation(out=za[t % 2][:, 0:T], in_=acc_a[:], func=ACT.Copy)
+
+        def heads_product(t):
+            acc_b = psum.tile([P, T], F32, name="acc_b", tag=b_bank[t])
+            nc.tensor.matmul_mx(
+                out=acc_b[:],
+                lhsT=b_codes[:, 2 * P * t : 2 * P * (t + 1)].bitcast(FP4X4),
+                lhsT_scale=b_plane[:, P * t : P * (t + 1)],
+                rhs=x_codes[:].bitcast(FP8X4),
+                rhs_scale=x_plane[:],
+                start=True,
+                stop=True,
+            )
+            nc.scalar.activation(out=zb[t % 2][:, 0:T], in_=acc_b[:], func=ACT.Copy)
+
+        def gather_tails(t):
+            tails[t] = keep.tile([P, J], F32, name="tails", tag=tails_slot[t])
+            nc.vector.tensor_copy(out=tails[t][:], in_=za[t % 2][:].indirect(tail_list[:]))
+
+        def edges(t):
+            diff = keep.tile([P, J], F32, name="diff", tag=diff_slot[t])
+            widths = [256,128,128] if t == TILES - 1 else [J]
+            j0 = 0
+            for i, w in enumerate(widths):
+                cols = slice(j0, j0 + w)
+                nc.vector.tensor_tensor(
+                    out=diff[:, cols],
+                    in0=zb[t % 2][:].indirect(head_list[:, j0 // 16 : (j0 + w) // 16]),
+                    in1=tails[t][:, cols],
+                    op=ALU.subtract,
+                )
+                size = keep.tile([P, w], F32, name=f"size{t}_{j0}")
+                nc.scalar.activation(out=size[:], in_=diff[:, cols], func=ACT.Abs)
+                root = keep.tile([P, w], F32, name=f"root{t}_{j0}")
+                nc.scalar.activation(out=root[:], in_=size[:], func=ACT.Abs_reciprocal_sqrt, bias=1.0)
+                soft = keep.tile([P, w], F32, name=f"soft{t}_{j0}")
+                (nc.gpsimd if t in [] else nc.vector).tensor_tensor(out=soft[:], in0=diff[:, cols], in1=root[:], op=ALU.mult)
+                energy = keep.tile([P, w], F32, name=f"energy{t}_{j0}")
+                if t == TILES - 1 and i in [2]:
+                    nc.vector.tensor_tensor(out=energy[:], in0=soft[:], in1=soft[:], op=ALU.mult)
+                else:
+                    nc.scalar.activation(out=energy[:], in_=soft[:], func=ACT.Square)
+                nc.sync.dma_start(out=out[P * t : P * (t + 1), cols], in_=energy[:])
+                j0 = j0 + w
+
+        for t in (0, 1):
+            tails_product(t)
+        for t in (0, 1):
+            heads_product(t)
+            gather_tails(t)
+        for t in (2, 3):
+            tails_product(t)
+        for t in (0, 1):
+            edges(t)
+            heads_product(t + 2)
+        for t in (2, 3):
+            gather_tails(t)
+            edges(t)

@@ -1,6 +1,7 @@
 from contextlib import ExitStack
 
 import concourse.mybir as mybir
+from concourse.masks import make_identity
 
 K, T, J, N = 512, 512, 512, 512
 FLOPS = 2 * 2 * K * N * T
@@ -20,7 +21,7 @@ P = 128
 PACK = 4
 TILES = N // P
 ZA_COLS = 704
-ZB_COLS = 1024
+ZB_COLS = 2048
 
 
 def load_scale_rows(queue, plane, rows):
@@ -45,7 +46,6 @@ def tile_list_edge_difference_energy_kernel(tc, xt_words, xt_scales, wa, wb_word
         nc.vector.memset(x_plane[:].bitcast(I32), 0)
         nc.vector.memset(b_plane[:].bitcast(I32), 0)
         nc.vector.memset(warm[:, 0:1], 1.0)
-        load_scale_rows(nc.scalar, x_plane, xt_scales[0])
         nc.scalar.activation(out=warm[:, 1:2], in_=warm[:, 0:1], func=ACT.Abs_reciprocal_sqrt)
 
         wa_rows = wa.rearrange("(p j) n -> p j n", j=PACK)
@@ -54,48 +54,56 @@ def tile_list_edge_difference_energy_kernel(tc, xt_words, xt_scales, wa, wb_word
         raw23 = keep.tile([P, PACK, 2 * P], F32, name="raw23")
         raws = [raw0[:], raw1[:], raw23[:, :, 0:P], raw23[:, :, P : 2 * P]]
         nc.sync.dma_start(out=raw0[:], in_=wa_rows[:, :, 0:P])
-        nc.sync.dma_start(out=tail_list[:], in_=offs)
+        load_scale_rows(nc.sync, x_plane, xt_scales[0])
         nc.sync.dma_start(out=x_codes[:].bitcast(I32), in_=xt_words[0].rearrange("p n t -> p (n t)").bitcast(I32))
         nc.sync.dma_start(out=raw1[:], in_=wa_rows[:, :, P : 2 * P])
         nc.sync.dma_start(out=raw23[:], in_=wa_rows[:, :, 2 * P : 4 * P])
+        nc.sync.dma_start(out=tail_list[:], in_=offs)
         load_scale_rows(nc.sync, b_plane, wb_scales[0])
         nc.sync.dma_start(out=b_codes[:].bitcast(I32), in_=wb_words[0].bitcast(I32))
         nc.sync.dma_start(out=head_list[:], in_=offs2)
 
-        za = [keep.tile([P, ZA_COLS], F32, name=f"za{w}") for w in range(2)]
-        zb = [keep.tile([P, ZB_COLS], F32, name=f"zb{w}") for w in range(2)]
-        for w in range(2):
-            nc.vector.memset(za[w][:, T:], 0.0)
-            nc.vector.memset(zb[w][:, T:], 0.0)
+        za = [keep.tile([P, ZA_COLS], F32, name=f"za{w}") for w in range(TILES)]
+        zb = [keep.tile([P, ZB_COLS if w < 2 else 1024], F32, name=f"zb{w}") for w in range(TILES)]
 
-        a_bank = ["p0", "p1", "p2", "p3"]
-        b_bank = ["p2", "p3", "p4", "p5"]
-        tails_slot = ["a", "b", "c", "c"]
-        diff_slot = ["c", "d", "d", "d"]
+        identity = keep.tile([P, P], F32, name="identity")
+        make_identity(nc, identity[:])
+        a_bank = ["p0","p1","p2","p3"]
+        b_bank = ["p2","p3","p0","p1"]
+        d_bank = ["p0","p1"]
+        e_bank = ["p4","p5"]
         tails = {}
+        heads = {}
 
         def tails_product(t):
             grouped = keep.tile([P, P, PACK], BF16, name=f"grouped{t}", align_bytes=64)
-            (nc.vector.tensor_copy if t in [0] else nc.scalar.copy)(
-                out=grouped[:].rearrange("p (c i) j -> p c j i", i=4),
-                in_=raws[t].rearrange("p j (c i) -> p c j i", i=4),
-            )
+            dealt = grouped[:].rearrange("p (c i) j -> p c j i", i=4)
+            source = raws[t].rearrange("p j (c i) -> p c j i", i=4)
+            if ["V","V","S","S"][t] == "V":
+                nc.vector.tensor_copy(out=dealt, in_=source)
+            elif ["V","V","S","S"][t] == "S":
+                nc.scalar.copy(out=dealt, in_=source)
+            else:
+                nc.gpsimd.tensor_scalar(out=dealt, in0=source, scalar1=1.0, scalar2=0.0, op0=ALU.mult, op1=ALU.add)
             a_codes = keep.tile([P, P], U32, name=f"a_codes{t}", align_bytes=64)
             a_plane = keep.tile([P, P], U8, name=f"a_plane{t}", align_bytes=64)
             nc.vector.quantize_mx(
                 out=a_codes[:].bitcast(FP8X4), scales=a_plane[:], in_=grouped[:].rearrange("p n j -> p (n j)")
             )
-            acc_a = psum.tile([P, T], F32, name="acc_a", tag=a_bank[t])
-            nc.tensor.matmul_mx(
-                out=acc_a[:],
-                lhsT=a_codes[:].bitcast(FP8X4),
-                lhsT_scale=a_plane[:],
-                rhs=x_codes[:].bitcast(FP8X4),
-                rhs_scale=x_plane[:],
-                start=True,
-                stop=True,
-            )
-            nc.scalar.activation(out=za[t % 2][:, 0:T], in_=acc_a[:], func=ACT.Copy)
+            halves = 2 if t < 2 else 1
+            for h in range(halves):
+                cols = slice(h * T // halves, (h + 1) * T // halves)
+                acc_a = psum.tile([P, T // halves], F32, name="acc_a", tag=a_bank[t] if h == 0 else f"p{6 + t}")
+                nc.tensor.matmul_mx(
+                    out=acc_a[:],
+                    lhsT=a_codes[:].bitcast(FP8X4),
+                    lhsT_scale=a_plane[:],
+                    rhs=x_codes[:, cols].bitcast(FP8X4),
+                    rhs_scale=x_plane[:, cols],
+                    start=True,
+                    stop=True,
+                )
+                nc.scalar.activation(out=za[t][:, cols], in_=acc_a[:], func=ACT.Copy)
 
         def heads_product(t):
             acc_b = psum.tile([P, T], F32, name="acc_b", tag=b_bank[t])
@@ -108,48 +116,100 @@ def tile_list_edge_difference_energy_kernel(tc, xt_words, xt_scales, wa, wb_word
                 start=True,
                 stop=True,
             )
-            nc.scalar.activation(out=zb[t % 2][:, 0:T], in_=acc_b[:], func=ACT.Copy)
+            nc.scalar.activation(out=zb[t][:, 0:T], in_=acc_b[:], func=ACT.Copy)
+
+        softs = {}
 
         def gather_tails(t):
-            tails[t] = keep.tile([P, J], F32, name="tails", tag=tails_slot[t])
-            nc.vector.tensor_copy(out=tails[t][:], in_=za[t % 2][:].indirect(tail_list[:]))
+            tails[t] = keep.tile([P, J], F32, name="tails", tag="root1" if t == TILES - 1 else f"tails{t}")
+            nc.vector.tensor_copy(out=tails[t][:], in_=za[t][:].indirect(tail_list[:]))
 
-        def edges(t):
-            diff = keep.tile([P, J], F32, name="diff", tag=diff_slot[t])
-            widths = [256,128,128] if t == TILES - 1 else [J]
-            j0 = 0
-            for i, w in enumerate(widths):
-                cols = slice(j0, j0 + w)
-                nc.vector.tensor_tensor(
-                    out=diff[:, cols],
-                    in0=zb[t % 2][:].indirect(head_list[:, j0 // 16 : (j0 + w) // 16]),
-                    in1=tails[t][:, cols],
-                    op=ALU.subtract,
-                )
-                size = keep.tile([P, w], F32, name=f"size{t}_{j0}")
-                nc.scalar.activation(out=size[:], in_=diff[:, cols], func=ACT.Abs)
-                root = keep.tile([P, w], F32, name=f"root{t}_{j0}")
-                nc.scalar.activation(out=root[:], in_=size[:], func=ACT.Abs_reciprocal_sqrt, bias=1.0)
-                soft = keep.tile([P, w], F32, name=f"soft{t}_{j0}")
-                (nc.gpsimd if t in [] else nc.vector).tensor_tensor(out=soft[:], in0=diff[:, cols], in1=root[:], op=ALU.mult)
-                energy = keep.tile([P, w], F32, name=f"energy{t}_{j0}")
-                if t == TILES - 1 and i in [2]:
-                    nc.vector.tensor_tensor(out=energy[:], in0=soft[:], in1=soft[:], op=ALU.mult)
-                else:
-                    nc.scalar.activation(out=energy[:], in_=soft[:], func=ACT.Square)
-                nc.sync.dma_start(out=out[P * t : P * (t + 1), cols], in_=energy[:])
-                j0 = j0 + w
+        def gather_heads(t):
+            heads[t] = keep.tile([P, J], F32, name=f"heads{t}")
+            nc.vector.tensor_scalar(
+                out=heads[t][:],
+                in0=zb[t][:].indirect(head_list[:]),
+                scalar1=-1.0,
+                scalar2=0.0,
+                op0=ALU.mult,
+                op1=ALU.add,
+            )
+
+        def soften(t, diff, w, label, size_tag):
+            size = keep.tile([P, w], F32, name="size", tag=size_tag)
+            nc.scalar.activation(out=size[:], in_=diff, func=ACT.Abs)
+            root = keep.tile([P, w], F32, name="root", tag=f"root{label}")
+            nc.scalar.activation(out=root[:], in_=size[:], func=ACT.Abs_reciprocal_sqrt, bias=1.0)
+            soft = keep.tile([P, w], F32, name=f"soft{label}")
+            if False and t == 0:
+                nc.gpsimd.tensor_tensor(out=soft[:], in0=size[:], in1=root[:], op=ALU.mult)
+            else:
+                nc.vector.tensor_tensor(out=soft[:], in0=diff, in1=root[:], op=ALU.mult)
+            return soft
+
+        def turned_edges(t):
+            diff = psum.tile([P, J], F32, name="diff", tag=d_bank[t])
+            for half, src in enumerate((tails[t], heads[t])):
+                for c in range(J // P):
+                    nc.tensor.matmul(
+                        out=diff[:, P * c : P * (c + 1)],
+                        lhsT=src[:, P * c : P * (c + 1)],
+                        rhs=identity[:],
+                        is_transpose=True,
+                        start=(half == 0 and c == 0),
+                        stop=(half == 1 and c == J // P - 1),
+                    )
+            softs[t] = soften(t, diff[:], J, t, "size")
+
+        def turn_back(t, energy):
+            back = psum.tile([P, J], F32, name="back", tag=e_bank[t])
+            for c in range(J // P):
+                nc.tensor.transpose(back[:, P * c : P * (c + 1)], softs[t][:, P * c : P * (c + 1)], identity[:])
+            nc.scalar.activation(out=energy, in_=back[:], func=ACT.Square)
+            nc.sync.dma_start(out=out[P * t : P * (t + 1), :], in_=energy)
+
+        def subtract(t, diff, j0, w):
+            nc.vector.tensor_tensor(
+                out=diff[:, j0 : j0 + w],
+                in0=zb[t][:].indirect(head_list[:, j0 // 16 : (j0 + w) // 16]),
+                in1=tails[t][:, j0 : j0 + w],
+                op=ALU.subtract,
+            )
+
+        def finish(t, soft, j0, w, on_vector):
+            energy = keep.tile([P, w], F32, name=f"energy{t}_{j0}")
+            if on_vector:
+                nc.vector.tensor_tensor(out=energy[:], in0=soft[:], in1=soft[:], op=ALU.mult)
+            else:
+                nc.scalar.activation(out=energy[:], in_=soft[:], func=ACT.Square)
+            nc.sync.dma_start(out=out[P * t : P * (t + 1), j0 : j0 + w], in_=energy[:])
 
         for t in (0, 1):
             tails_product(t)
         for t in (0, 1):
             heads_product(t)
             gather_tails(t)
+        for t in (0, 1):
+            gather_heads(t)
+        for t in (2, 3):
+            heads_product(t)
         for t in (2, 3):
             tails_product(t)
         for t in (0, 1):
-            edges(t)
-            heads_product(t + 2)
-        for t in (2, 3):
-            gather_tails(t)
-            edges(t)
+            turned_edges(t)
+        gather_tails(2)
+        diff2 = keep.tile([P, J], F32, name="diff2")
+        subtract(2, diff2, 0, J)
+        soft2 = soften(2, diff2[:], J, 2, "size")
+        pair = keep.tile([P, 2, J], F32, name="pair", tag="size")
+        for t in (0, 1):
+            turn_back(t, pair[:, t, :])
+        finish(2, soft2, 0, J, False)
+        gather_tails(3)
+        diff3 = keep.tile([P, J], F32, name="diff3", tag="root2")
+        j0 = 0
+        for i, w in enumerate([256,128,128]):
+            subtract(3, diff3, j0, w)
+            soft3 = soften(3, diff3[:, j0 : j0 + w], w, f"3_{j0}", f"size3_{j0}")
+            finish(3, soft3, j0, w, i in [])
+            j0 = j0 + w

@@ -67,7 +67,8 @@ def tile_list_edge_difference_energy_kernel(tc, xt_words, xt_scales, wa, wb_word
         zb = [keep.tile([P, ZB_COLS if w < 2 else 1024], F32, name=f"zb{w}") for w in range(TILES)]
 
         identity = keep.tile([P, P], F32, name="identity")
-        make_identity(nc, identity[:])
+        nc.vector.memset(identity[:], 0.0)
+        make_identity(nc, identity[:], nomemset=True)
         a_bank = ["p0","p1","p2","p3"]
         b_bank = ["p2","p3","p0","p1"]
         d_bank = ["p0","p1"]

from contextlib import ExitStack

import concourse.mybir as mybir
from concourse.masks import make_identity

K, T, J, N = 512, 512, 512, 512
FLOPS = 2 * 2 * K * N * T

F32 = mybir.dt.float32
BF16 = mybir.dt.bfloat16
I32 = mybir.dt.int32
U32 = mybir.dt.uint32
U16 = mybir.dt.uint16
U8 = mybir.dt.uint8
FP8X4 = mybir.dt.float8_e4m3fn_x4
FP4X4 = mybir.dt.float4_e2m1fn_x4
ACT = mybir.ActivationFunctionType
ALU = mybir.AluOpType

P = 128
PACK = 4
TILES = N // P
ZA_COLS = 704
ZB_COLS = 2048


def load_scale_rows(queue, plane, rows):
    for q in range(4):
        queue.dma_start(out=plane[32 * q : 32 * q + 4, :].bitcast(I32), in_=rows[4 * q : 4 * q + 4, :].bitcast(I32))


def tile_list_edge_difference_energy_kernel(tc, xt_words, xt_scales, wa, wb_words, wb_scales, offs, offs2, out):
    nc = tc.nc
    with ExitStack() as ctx:
        keep = ctx.enter_context(tc.tile_pool(name="keep", bufs=1))
        psum = ctx.enter_context(tc.psum_pool(name="psum", bufs=1))

        tail_list = keep.tile([P, J // 16], U16, name="tail_list")
        head_list = keep.tile([P, J // 16], U16, name="head_list")
        x_codes = keep.tile([P, T], U32, name="x_codes", align_bytes=64)
        x_plane = keep.tile([P, T], U8, name="x_plane", align_bytes=64)
        b_codes = keep.tile([P, 2 * N], U8, name="b_codes", align_bytes=64)
        b_plane = keep.tile([P, N], U8, name="b_plane", align_bytes=64)
        warm = keep.tile([P, 2], F32, name="warm")

        nc.vector.memset(x_plane[:].bitcast(I32), 0)
        nc.vector.memset(b_plane[:].bitcast(I32), 0)
        nc.vector.memset(warm[:, 0:1], 1.0)
        nc.scalar.activation(out=warm[:, 1:2], in_=warm[:, 0:1], func=ACT.Abs_reciprocal_sqrt)

        wa_rows = wa.rearrange("(p j) n -> p j n", j=PACK)
        raw0 = keep.tile([P, PACK, P], F32, name="raw0")
        raw1 = keep.tile([P, PACK, P], F32, name="raw1")
        raw23 = keep.tile([P, PACK, 2 * P], F32, name="raw23")
        raws = [raw0[:], raw1[:], raw23[:, :, 0:P], raw23[:, :, P : 2 * P]]
        nc.sync.dma_start(out=raw0[:], in_=wa_rows[:, :, 0:P])
        load_scale_rows(nc.sync, x_plane, xt_scales[0])
        nc.sync.dma_start(out=x_codes[:].bitcast(I32), in_=xt_words[0].rearrange("p n t -> p (n t)").bitcast(I32))
        nc.sync.dma_start(out=raw1[:], in_=wa_rows[:, :, P : 2 * P])
        nc.sync.dma_start(out=raw23[:], in_=wa_rows[:, :, 2 * P : 4 * P])
        nc.sync.dma_start(out=tail_list[:], in_=offs)
        load_scale_rows(nc.sync, b_plane, wb_scales[0])
        nc.sync.dma_start(out=b_codes[:].bitcast(I32), in_=wb_words[0].bitcast(I32))
        nc.sync.dma_start(out=head_list[:], in_=offs2)

        za = [keep.tile([P, ZA_COLS], F32, name=f"za{w}") for w in range(TILES)]
        zb = [keep.tile([P, ZB_COLS if w < 2 else 1024], F32, name=f"zb{w}") for w in range(TILES)]

        identity = keep.tile([P, P], F32, name="identity")
        nc.vector.memset(identity[:], 0.0)
        make_identity(nc, identity[:], nomemset=True)
        a_bank = ["p0","p1","p2","p3"]
        b_bank = ["p2","p3","p0","p1"]
        d_bank = ["p0","p1"]
        e_bank = ["p4","p5"]
        tails = {}
        heads = {}

        def tails_product(t):
            grouped = keep.tile([P, P, PACK], BF16, name=f"grouped{t}", align_bytes=64)
            dealt = grouped[:].rearrange("p (c i) j -> p c j i", i=4)
            source = raws[t].rearrange("p j (c i) -> p c j i", i=4)
            if ["V","V","S","S"][t] == "V":
                nc.vector.tensor_copy(out=dealt, in_=source)
            elif ["V","V","S","S"][t] == "S":
                nc.scalar.copy(out=dealt, in_=source)
            else:
                nc.gpsimd.tensor_scalar(out=dealt, in0=source, scalar1=1.0, scalar2=0.0, op0=ALU.mult, op1=ALU.add)
            a_codes = keep.tile([P, P], U32, name=f"a_codes{t}", align_bytes=64)
            a_plane = keep.tile([P, P], U8, name=f"a_plane{t}", align_bytes=64)
            nc.vector.quantize_mx(
                out=a_codes[:].bitcast(FP8X4), scales=a_plane[:], in_=grouped[:].rearrange("p n j -> p (n j)")
            )
            halves = 2 if t < 2 else 1
            for h in range(halves):
                cols = slice(h * T // halves, (h + 1) * T // halves)
                acc_a = psum.tile([P, T // halves], F32, name="acc_a", tag=a_bank[t] if h == 0 else f"p{6 + t}")
                nc.tensor.matmul_mx(
                    out=acc_a[:],
                    lhsT=a_codes[:].bitcast(FP8X4),
                    lhsT_scale=a_plane[:],
                    rhs=x_codes[:, cols].bitcast(FP8X4),
                    rhs_scale=x_plane[:, cols],
                    start=True,
                    stop=True,
                )
                nc.scalar.activation(out=za[t][:, cols], in_=acc_a[:], func=ACT.Copy)

        def heads_product(t):
            acc_b = psum.tile([P, T], F32, name="acc_b", tag=b_bank[t])
            nc.tensor.matmul_mx(
                out=acc_b[:],
                lhsT=b_codes[:, 2 * P * t : 2 * P * (t + 1)].bitcast(FP4X4),
                lhsT_scale=b_plane[:, P * t : P * (t + 1)],
                rhs=x_codes[:].bitcast(FP8X4),
                rhs_scale=x_plane[:],
                start=True,
                stop=True,
            )
            nc.scalar.activation(out=zb[t][:, 0:T], in_=acc_b[:], func=ACT.Copy)

        softs = {}

        def gather_tails(t):
            tails[t] = keep.tile([P, J], F32, name="tails", tag="root1" if t == TILES - 1 else f"tails{t}")
            nc.vector.tensor_copy(out=tails[t][:], in_=za[t][:].indirect(tail_list[:]))

        def gather_heads(t):
            heads[t] = keep.tile([P, J], F32, name=f"heads{t}")
            nc.vector.tensor_scalar(
                out=heads[t][:],
                in0=zb[t][:].indirect(head_list[:]),
                scalar1=-1.0,
                scalar2=0.0,
                op0=ALU.mult,
                op1=ALU.add,
            )

        def soften(t, diff, w, label, size_tag):
            size = keep.tile([P, w], F32, name="size", tag=size_tag)
            nc.scalar.activation(out=size[:], in_=diff, func=ACT.Abs)
            root = keep.tile([P, w], F32, name="root", tag=f"root{label}")
            nc.scalar.activation(out=root[:], in_=size[:], func=ACT.Abs_reciprocal_sqrt, bias=1.0)
            soft = keep.tile([P, w], F32, name=f"soft{label}")
            if False and t == 0:
                nc.gpsimd.tensor_tensor(out=soft[:], in0=size[:], in1=root[:], op=ALU.mult)
            else:
                nc.vector.tensor_tensor(out=soft[:], in0=diff, in1=root[:], op=ALU.mult)
            return soft

        def turned_edges(t):
            diff = psum.tile([P, J], F32, name="diff", tag=d_bank[t])
            for half, src in enumerate((tails[t], heads[t])):
                for c in range(J // P):
                    nc.tensor.matmul(
                        out=diff[:, P * c : P * (c + 1)],
                        lhsT=src[:, P * c : P * (c + 1)],
                        rhs=identity[:],
                        is_transpose=True,
                        start=(half == 0 and c == 0),
                        stop=(half == 1 and c == J // P - 1),
                    )
            softs[t] = soften(t, diff[:], J, t, "size")

        def turn_back(t, energy):
            back = psum.tile([P, J], F32, name="back", tag=e_bank[t])
            for c in range(J // P):
                nc.tensor.transpose(back[:, P * c : P * (c + 1)], softs[t][:, P * c : P * (c + 1)], identity[:])
            nc.scalar.activation(out=energy, in_=back[:], func=ACT.Square)
            nc.sync.dma_start(out=out[P * t : P * (t + 1), :], in_=energy)

        def subtract(t, diff, j0, w):
            nc.vector.tensor_tensor(
                out=diff[:, j0 : j0 + w],
                in0=zb[t][:].indirect(head_list[:, j0 // 16 : (j0 + w) // 16]),
                in1=tails[t][:, j0 : j0 + w],
                op=ALU.subtract,
            )

        def finish(t, soft, j0, w, on_vector):
            energy = keep.tile([P, w], F32, name=f"energy{t}_{j0}")
            if on_vector:
                nc.vector.tensor_tensor(out=energy[:], in0=soft[:], in1=soft[:], op=ALU.mult)
            else:
                nc.scalar.activation(out=energy[:], in_=soft[:], func=ACT.Square)
            nc.sync.dma_start(out=out[P * t : P * (t + 1), j0 : j0 + w], in_=energy[:])

        for t in (0, 1):
            tails_product(t)
        for t in (0, 1):
            heads_product(t)
            gather_tails(t)
        for t in (0, 1):
            gather_heads(t)
        for t in (2, 3):
            heads_product(t)
        for t in (2, 3):
            tails_product(t)
        for t in (0, 1):
            turned_edges(t)
        gather_tails(2)
        diff2 = keep.tile([P, J], F32, name="diff2")
        subtract(2, diff2, 0, J)
        soft2 = soften(2, diff2[:], J, 2, "size")
        pair = keep.tile([P, 2, J], F32, name="pair", tag="size")
        for t in (0, 1):
            turn_back(t, pair[:, t, :])
        finish(2, soft2, 0, J, False)
        gather_tails(3)
        diff3 = keep.tile([P, J], F32, name="diff3", tag="root2")
        j0 = 0
        for i, w in enumerate([256,128,128]):
            subtract(3, diff3, j0, w)
            soft3 = soften(3, diff3[:, j0 : j0 + w], w, f"3_{j0}", f"size3_{j0}")
            finish(3, soft3, j0, w, i in [])
            j0 = j0 + w
